import numpy as np
import ml_dtypes


def mxq(x, axis, fmt="e4m3"):
    dtype, down = {"e4m3": (ml_dtypes.float8_e4m3fn, 7), "e5m2": (ml_dtypes.float8_e5m2, 14)}[fmt]
    v = np.moveaxis(np.asarray(x, np.float32).astype(ml_dtypes.bfloat16).astype(np.float64), axis, -1)
    blocks = v.reshape(v.shape[:-1] + (-1, 32))
    amax = np.abs(blocks).max(-1, keepdims=True)
    byte = np.maximum(np.where(amax > 0, np.frexp(amax)[1] - 1 + 127, 0) - down, 1)
    scale = np.exp2(byte - 127.0)
    codes = (blocks / scale).astype(np.float32).astype(dtype).astype(np.float64)
    return np.moveaxis((codes * scale).reshape(v.shape), -1, axis)


WIDE = False


def mx_kscale(k):
    if not WIDE:
        return np.ones(k)
    levels = np.array([10, -10, 5, -5, 0])
    if k % 512:
        return np.exp2(np.random.permutation(np.resize(levels, k // 32))).repeat(32)
    a = np.empty((k // 512, 16))
    for p in range(k // 512):
        a[p, :8] = np.random.permutation(np.resize(levels, 8))
        for g in range(8):
            far = levels[np.abs(levels - a[p, g]) >= 10]
            a[p, g + 8] = far[np.random.randint(len(far))]
    return np.exp2(a.ravel()).repeat(32)


def f64(x):
    return np.asarray(x).astype(np.float64)


def striped(idx):
    return np.tile(idx.reshape(-1, 16).T, (8, 1)).astype(np.uint16)


def unstriped(offs):
    return offs[:16].T.reshape(-1).astype(np.int64)


def pack_weight(w):
    k, n = w.shape
    w = f64(np.asarray(w, np.float32).astype(ml_dtypes.bfloat16)).reshape(k // 32, 32, n)
    amax = np.abs(w).max(1)
    byte = np.clip(np.where(amax > 0, np.frexp(amax)[1] - 1 + 127 - 7, 1), 1, 254)
    scaled = (w * np.exp2(127.0 - byte)[:, None, :]).reshape(k, n).astype(np.float32)
    words = np.ascontiguousarray(scaled.reshape(k // 512, 128, 4, n).transpose(0, 1, 3, 2)).astype(ml_dtypes.float8_e4m3fn).view(np.uint8)
    return words, np.ascontiguousarray(byte.astype(np.uint8).reshape(k // 512, 16, n))


def unpack_weight(words, scales):
    g, p, n, _ = words.shape
    vals = np.ascontiguousarray(words).view(ml_dtypes.float8_e4m3fn).astype(np.float64) * np.repeat(np.exp2(scales.astype(np.float64) - 127.0), 8, axis=1)[..., None]
    return vals.transpose(0, 1, 3, 2).reshape(g * 512, n)


def sigmoid(v):
    return 1.0 / (1.0 + np.exp(-np.maximum(v, -700.0)))


K, T, S, N, H = 512, 2048, 512, 512, 512


def setup_inputs():
    n = np.random.standard_normal
    s = mx_kscale(K)[:, None]
    u = mx_kscale(H)
    packed_xT = pack_weight(n((K, T)) * s)
    return {
        "x_words": packed_xT[0],
        "x_scales": packed_xT[1],
        "w1": (n((K, H)) / np.sqrt(K) / s).astype(np.float32),
        "tau": np.random.uniform(0.3, 0.9, (H, 1)).astype(np.float32),
        "sl": np.random.uniform(1.0, 2.0, (H, 1)).astype(np.float32),
        "th": (0.5 * n((H, 1))).astype(np.float32),
        "gn": (np.random.uniform(0.5, 1.5, (H, 1)) * u[:, None]).astype(np.float32),
        "w2": (n((H, N)) / np.sqrt(H) / u[:, None]).astype(np.float32),
        "gm": (np.random.uniform(0.5, 1.5, (H, 1)) * u[:, None]).astype(np.float32),
        "w3": (n((H, N)) / np.sqrt(H) / u[:, None]).astype(np.float32),
        "sl2": np.random.uniform(1.0, 2.0, (N, 1)).astype(np.float32),
        "th2": (0.5 * n((N, 1))).astype(np.float32),
        "sl3": np.random.uniform(1.0, 2.0, (N, 1)).astype(np.float32),
        "th3": (0.5 * n((N, 1))).astype(np.float32),
        "offs": striped(np.random.permutation(T)[:S]),
        "n1": striped(np.random.permutation(S)),
        "n2": striped(np.random.permutation(S)),
        "n3": striped(np.random.permutation(S)),
        "n4": striped(np.random.permutation(S)),
        "n5": striped(np.random.permutation(S)),
        "n6": striped(np.random.permutation(S)),
    }


def reference(x_words, x_scales, w1, tau, sl, th, gn, w2, gm, w3, sl2, th2, sl3, th3, offs, n1, n2, n3, n4, n5, n6):
    xq = unpack_weight(x_words, x_scales)[:, unstriped(offs)]
    y = mxq(f64(w1), 0, "e4m3").T @ xq
    sq = (y) ** 2
    ea = np.exp(-1.0 * (f64(tau) * sq[:, unstriped(n1)]))
    z = f64(gn) * (y * ea - (0.5 * y[:, unstriped(n2)]))
    a = mxq(f64(w2), 0, "e4m3").T @ mxq(z, 0, "e4m3")
    sg2 = sigmoid(f64(sl2) * (a[:, unstriped(n5)] - f64(th2)))
    pa = y[:, unstriped(n3)]
    sg = sigmoid(f64(sl) * (y[:, unstriped(n4)] - f64(th)))
    z2 = f64(gm) * (pa + sg * (y - pa))
    b = mxq(f64(w3), 0, "e4m3").T @ mxq(z2, 0, "e4m3")
    sg3 = sigmoid(f64(sl3) * (b[:, unstriped(n6)] - f64(th3)))
    return sg2 * b + sg3 * a

@@ -1,0 +1,240 @@
+from contextlib import ExitStack
+
+import concourse.mybir as mybir
+
+F32 = mybir.dt.float32
+BF16 = mybir.dt.bfloat16
+I32 = mybir.dt.int32
+U32 = mybir.dt.uint32
+U16 = mybir.dt.uint16
+U8 = mybir.dt.uint8
+FP8X4 = mybir.dt.float8_e4m3fn_x4
+ALU = mybir.AluOpType
+ACT = mybir.ActivationFunctionType
+
+P = 128
+PACK = 4
+T = 2048
+S = 512
+HALF = S // 2
+LIST_COLS = S // 16
+RUN = 4
+FLOPS = 3 * 2 * 512 * 512 * 512
+
+
+def tile_picked_forkcxbegaebl_none_p_kernel(
+    tc, x_words, x_scales, w1, tau, sl, th, gn, w2, gm, w3, sl2, th2, sl3, th3, offs, n1, n2, n3, n4, n5, n6, out
+):
+    nc = tc.nc
+    halves = [slice(h * HALF, (h + 1) * HALF) for h in range(2)]
+    list_halves = [slice(h * LIST_COLS // 2, (h + 1) * LIST_COLS // 2) for h in range(2)]
+
+    with ExitStack() as ctx:
+        lists = ctx.enter_context(tc.tile_pool(name="lists", bufs=1))
+        keep = ctx.enter_context(tc.tile_pool(name="keep", bufs=1))
+        psum = ctx.enter_context(tc.psum_pool(name="psum", bufs=1))
+
+        def load_list(dram, name):
+            tile = lists.tile([P, LIST_COLS], U16, name=name)
+            nc.sync.dma_start(tile[:], dram)
+            return tile
+
+        def load_weight(dram, name):
+            raw = keep.tile([P, PACK, S], F32, name=name + "_raw")
+            nc.sync.dma_start(raw[:], dram.rearrange("(p j) c -> p j c", j=PACK))
+            return raw
+
+        def load_rows(engine, dst, dram):
+            engine.dma_start(dst, dram.rearrange("(p t) one -> p (t one)", t=PACK))
+
+        def weave_weight(raw, name):
+            woven = keep.tile([P, PACK * S], BF16, name=name + "_bf16", align_bytes=64)
+            nc.vector.tensor_copy(
+                out=woven[:].rearrange("p (t m j) -> p m j t", t=PACK, j=PACK),
+                in_=raw[:].rearrange("p j (m t) -> p m j t", t=PACK),
+            )
+            return woven
+
+        def quantize(woven, name):
+            width = woven.shape[1] // PACK
+            codes = keep.tile([P, width], U32, name=name + "_codes", align_bytes=64)
+            scales = keep.tile([P, width], U8, name=name + "_scales", align_bytes=64)
+            nc.vector.quantize_mx(out=codes[:].bitcast(FP8X4), scales=scales[:], in_=woven[:])
+            return codes, scales
+
+        def product(bank, weight, t, h, codes, scales):
+            cols = slice(t * P, (t + 1) * P)
+            nc.tensor.matmul_mx(
+                out=bank[:, halves[h]],
+                lhsT=weight[0][:, cols].bitcast(FP8X4),
+                lhsT_scale=weight[1][:, cols],
+                rhs=codes.bitcast(FP8X4),
+                rhs_scale=scales,
+                start=True,
+                stop=True,
+            )
+
+        def by_runs(planes, h):
+            return planes[:, :, halves[h]].rearrange("p t (c i) -> p c t i", i=RUN)
+
+        def woven_runs(woven):
+            return woven[:].rearrange("p (c i t) -> p c t i", i=RUN, t=PACK)
+
+        def planes4(name):
+            return [keep.tile([P, S], F32, name="%s%d" % (name, t)) for t in range(PACK)]
+
+        xs = keep.tile([P, T], U8, name="xs")
+        nc.vector.memset(xs[:].bitcast(I32), 0)
+        offs_t = load_list(offs, "offs_t")
+        w1_raw = load_weight(w1, "w1")
+        for q in range(4):
+            nc.sync.dma_start(xs[32 * q : 32 * q + 4, :].bitcast(I32), x_scales[0, 4 * q : 4 * q + 4, :].bitcast(I32))
+        xw = keep.tile([P, T], U32, name="xw")
+        nc.sync.dma_start(xw[:].bitcast(I32), x_words[0].rearrange("p c r -> p (c r)").bitcast(I32))
+        tau_t = keep.tile([P, PACK], F32, name="tau_t")
+        load_rows(nc.scalar, tau_t[:], tau)
+        n1_t = load_list(n1, "n1_t")
+        w2_raw = load_weight(w2, "w2")
+        n2_t = load_list(n2, "n2_t")
+        w3_raw = load_weight(w3, "w3")
+        n4_t = load_list(n4, "n4_t")
+        n3_t = load_list(n3, "n3_t")
+        gn_t = keep.tile([P, PACK], F32, name="gn_t")
+        gm_t = keep.tile([P, PACK], F32, name="gm_t")
+        load_rows(nc.sync, gn_t[:], gn)
+        load_rows(nc.sync, gm_t[:], gm)
+        slopes = keep.tile([P, 3, 8], F32, name="slopes")
+        thresholds = keep.tile([P, 3, 8], F32, name="thresholds")
+        for g, (slope, threshold) in enumerate(((sl, th), (sl2, th2), (sl3, th3))):
+            load_rows(nc.sync, slopes[:, g, 0:PACK], slope)
+            load_rows(nc.sync, thresholds[:, g, 0:PACK], threshold)
+        n5_t = load_list(n5, "n5_t")
+        n6_t = load_list(n6, "n6_t")
+
+        neg_tau = keep.tile([P, PACK], F32, name="neg_tau")
+        nc.scalar.activation(out=neg_tau[:], in_=tau_t[:], func=ACT.Copy, scale=-1.0)
+        neg_half_gn = keep.tile([P, PACK], F32, name="neg_half_gn")
+        nc.gpsimd.tensor_scalar(neg_half_gn[:], gn_t[:], -0.5, 0.0, ALU.mult, ALU.add)
+        neg_gm = keep.tile([P, PACK], F32, name="neg_gm")
+        nc.gpsimd.tensor_scalar(neg_gm[:], gm_t[:], -1.0, 0.0, ALU.mult, ALU.add)
+        neg_th = keep.tile([P, 3, PACK], F32, name="neg_th")
+        nc.gpsimd.tensor_scalar(neg_th[:], thresholds[:, :, 0:PACK], -1.0, 0.0, ALU.mult, ALU.add)
+        biases = keep.tile([P, 3, PACK], F32, name="biases")
+        nc.gpsimd.tensor_tensor(biases[:], neg_th[:], slopes[:, :, 0:PACK], ALU.mult)
+
+        def gated(dst, window, offsets, g, t, h):
+            nc.scalar.activation(
+                out=dst,
+                in_=window[:].indirect(offsets[:, list_halves[h]]),
+                func=ACT.Sigmoid,
+                scale=slopes[:, g, t : t + 1],
+                bias=biases[:, g, t : t + 1],
+            )
+
+        w1_woven = weave_weight(w1_raw, "w1")
+        xs_g = keep.tile([P, S], U8, name="xs_g", align_bytes=64)
+        nc.vector.tensor_copy(xs_g[:], xs[:].indirect(offs_t[:]))
+        w1_q = quantize(w1_woven, "w1")
+        xw_g = keep.tile([P, S], U32, name="xw_g", align_bytes=64)
+        low_banks = [psum.tile([P, S], F32, name="y_bank%d" % t, tag="low%d" % t) for t in range(PACK)]
+        for h in range(2):
+            nc.vector.tensor_copy(xw_g[:, halves[h]], xw[:].indirect(offs_t[:, list_halves[h]]))
+        for t in range(PACK):
+            for h in range(2):
+                product(low_banks[t], w1_q, t, h, xw_g[:, halves[h]], xs_g[:, halves[h]])
+
+        y = planes4("y")
+        ea = planes4("ea")
+        u = planes4("u")
+        d = keep.tile([P, PACK, S], F32, name="d")
+        weight_raw = [w2_raw, w3_raw]
+        weight_woven = []
+        weight_q = []
+        for t in range(PACK):
+            sq = keep.tile([P, S], F32, name="sq%d" % t, tag="sq%d" % t)
+            nc.scalar.activation(out=sq[:], in_=low_banks[t][:], func=ACT.Square)
+            nc.scalar.copy(y[t][:], low_banks[t][:])
+            for h in range(2):
+                nc.scalar.activation(
+                    out=ea[t][:, halves[h]],
+                    in_=sq[:].indirect(n1_t[:, list_halves[h]]),
+                    func=ACT.Exp,
+                    scale=neg_tau[:, t : t + 1],
+                )
+            if t % 2 == 0:
+                weight_woven.append(weave_weight(weight_raw[t // 2], "w%d" % (2 + t // 2)))
+            else:
+                weight_q.append(quantize(weight_woven[t // 2], "w%d" % (2 + t // 2)))
+            for h in range(2):
+                nc.vector.scalar_tensor_tensor(
+                    u[t][:, halves[h]], low_banks[t][:, halves[h]], 2.0, ea[t][:, halves[h]], ALU.mult, ALU.mult
+                )
+            for h in range(2):
+                nc.vector.tensor_tensor(
+                    d[:, t, halves[h]], y[t][:].indirect(n2_t[:, list_halves[h]]), u[t][:, halves[h]], ALU.subtract
+                )
+        w2_q, w3_q = weight_q
+
+        gain_runs = neg_half_gn[:].unsqueeze(1).unsqueeze(3).to_broadcast([P, HALF // RUN, PACK, RUN])
+        z_woven = [keep.tile([P, PACK * HALF], BF16, name="z_woven%d" % h, align_bytes=64) for h in range(2)]
+        for h in range(2):
+            nc.vector.tensor_tensor(woven_runs(z_woven[h]), by_runs(d, h), gain_runs, ALU.mult)
+        high_banks = [psum.tile([P, S], F32, name="a_bank%d" % t, tag="high%d" % t) for t in range(PACK)]
+        z_q = [quantize(z_woven[h], "z%d" % h) for h in range(2)]
+        for t in range(PACK):
+            for h in range(2):
+                product(high_banks[t], w2_q, t, h, z_q[h][0][:], z_q[h][1][:])
+
+        sg = keep.tile([P, PACK, S], F32, name="sg", tag="sq%d" % (PACK - 1))
+        r = planes4("r")
+        v = keep.tile([P, PACK, S], F32, name="v")
+        q = keep.tile([P, PACK, S], F32, name="q")
+        for t in range(PACK):
+            for h in range(2):
+                gated(sg[:, t, halves[h]], y[t], n4_t, 0, t, h)
+            nc.scalar.activation(
+                out=r[t][:], in_=sg[:, t, :], func=ACT.Identity, scale=neg_gm[:, t : t + 1], bias=gm_t[:, t : t + 1]
+            )
+            nc.vector.scalar_tensor_tensor(
+                v[:, t, :], low_banks[t][:], gm_t[:, t : t + 1], sg[:, t, :], ALU.mult, ALU.mult
+            )
+            for h in range(2):
+                nc.vector.tensor_tensor(
+                    q[:, t, halves[h]], y[t][:].indirect(n3_t[:, list_halves[h]]), r[t][:, halves[h]], ALU.mult
+                )
+
+        a = planes4("a")
+        sg2 = planes4("sg2")
+        for t in range(PACK):
+            nc.scalar.copy(a[t][:], high_banks[t][:])
+            for h in range(2):
+                gated(sg2[t][:, halves[h]], a[t], n5_t, 1, t, h)
+
+        z2_woven = [keep.tile([P, PACK * HALF], BF16, name="z2_woven%d" % h, align_bytes=64) for h in range(2)]
+        for h in range(2):
+            nc.vector.tensor_tensor(woven_runs(z2_woven[h]), by_runs(q, h), by_runs(v, h), ALU.add)
+        b_banks = [psum.tile([P, S], F32, name="b_bank%d" % t, tag="low%d" % t) for t in range(PACK)]
+        z2_q = [quantize(z2_woven[h], "z2_%d" % h) for h in range(2)]
+        for t in range(PACK):
+            for h in range(2):
+                product(b_banks[t], w3_q, t, h, z2_q[h][0][:], z2_q[h][1][:])
+
+        b = planes4("b")
+        sg3 = planes4("sg3")
+        left = planes4("left")
+        right = planes4("right")
+        res = planes4("res")
+        out_rows = out.rearrange("(p t) n -> p t n", t=PACK)
+        nc.scalar.copy(b[0][:], b_banks[0][:])
+        for t in (1, 0, 2, 3):
+            nc.vector.tensor_tensor(left[t][:], b_banks[t][:], sg2[t][:], ALU.mult)
+        for t in range(PACK):
+            if t + 1 < PACK:
+                nc.scalar.copy(b[t + 1][:], b_banks[t + 1][:])
+            for h in range(2):
+                gated(sg3[t][:, halves[h]], b[t], n6_t, 2, t, h)
+            pieces = halves if t == PACK - 1 else [slice(0, S)]
+            for cols in pieces:
+                nc.vector.tensor_tensor(right[t][:, cols], high_banks[t][:, cols], sg3[t][:, cols], ALU.mult)
+                nc.vector.tensor_tensor(res[t][:, cols], left[t][:, cols], right[t][:, cols], ALU.add)
+                nc.sync.dma_start(out_rows[:, t, cols], res[t][:, cols])

@@ -83,12 +83,20 @@ def tile_picked_forkcxbegaebl_none_p_kernel(
         def planes4(name):
             return [keep.tile([P, S], F32, name="%s%d" % (name, t)) for t in range(PACK)]
 
+        def pairs4(name):
+            return [keep.tile([P, 2 * S], F32, name="%s%d" % (name, t)) for t in range(PACK)]
+
+        def pieces(t):
+            if t == PACK - 1:
+                return list(zip(halves, list_halves))
+            return [(slice(0, S), slice(0, LIST_COLS))]
+
         xs = keep.tile([P, T], U8, name="xs")
-        nc.vector.memset(xs[:].bitcast(I32), 0)
+        nc.gpsimd.memset(xs[:].bitcast(I32), 0)
         offs_t = load_list(offs, "offs_t")
-        w1_raw = load_weight(w1, "w1")
         for q in range(4):
             nc.sync.dma_start(xs[32 * q : 32 * q + 4, :].bitcast(I32), x_scales[0, 4 * q : 4 * q + 4, :].bitcast(I32))
+        w1_raw = load_weight(w1, "w1")
         xw = keep.tile([P, T], U32, name="xw")
         nc.sync.dma_start(xw[:].bitcast(I32), x_words[0].rearrange("p c r -> p (c r)").bitcast(I32))
         tau_t = keep.tile([P, PACK], F32, name="tau_t")
@@ -122,19 +130,18 @@ def tile_picked_forkcxbegaebl_none_p_kernel(
         biases = keep.tile([P, 3, PACK], F32, name="biases")
         nc.gpsimd.tensor_tensor(biases[:], neg_th[:], slopes[:, :, 0:PACK], ALU.mult)
 
-        def gated(dst, window, offsets, g, t, h):
+        def gated(dst, window, offsets, g, t):
             nc.scalar.activation(
                 out=dst,
-                in_=window[:].indirect(offsets[:, list_halves[h]]),
+                in_=window[:].indirect(offsets),
                 func=ACT.Sigmoid,
                 scale=slopes[:, g, t : t + 1],
                 bias=biases[:, g, t : t + 1],
             )
 
-        w1_woven = weave_weight(w1_raw, "w1")
         xs_g = keep.tile([P, S], U8, name="xs_g", align_bytes=64)
         nc.vector.tensor_copy(xs_g[:], xs[:].indirect(offs_t[:]))
-        w1_q = quantize(w1_woven, "w1")
+        w1_q = quantize(weave_weight(w1_raw, "w1"), "w1")
         xw_g = keep.tile([P, S], U32, name="xw_g", align_bytes=64)
         low_banks = [psum.tile([P, S], F32, name="y_bank%d" % t, tag="low%d" % t) for t in range(PACK)]
         for h in range(2):
@@ -143,40 +150,49 @@ def tile_picked_forkcxbegaebl_none_p_kernel(
             for h in range(2):
                 product(low_banks[t], w1_q, t, h, xw_g[:, halves[h]], xs_g[:, halves[h]])
 
-        y = planes4("y")
-        ea = planes4("ea")
-        u = planes4("u")
+        y_ea = pairs4("y_ea")
+        a_u = pairs4("a_u")
+        b_sg2 = pairs4("b_sg2")
+        y = [pair[:, 0:S] for pair in y_ea]
+        ea = [pair[:, S : 2 * S] for pair in y_ea]
+        a = [pair[:, 0:S] for pair in a_u]
+        u = [pair[:, S : 2 * S] for pair in a_u]
+        b = [pair[:, 0:S] for pair in b_sg2]
+        sg2 = [pair[:, S : 2 * S] for pair in b_sg2]
         d = keep.tile([P, PACK, S], F32, name="d")
-        weight_raw = [w2_raw, w3_raw]
-        weight_woven = []
-        weight_q = []
+        sq = [keep.tile([P, S], F32, name="sq%d" % t, tag="sq%d" % t) for t in range(PACK)]
+
+        def square(t):
+            nc.scalar.activation(out=sq[t][:], in_=low_banks[t][:], func=ACT.Square)
+
+        def decay(t, h):
+            nc.scalar.activation(
+                out=ea[t][:, halves[h]],
+                in_=sq[t][:].indirect(n1_t[:, list_halves[h]]),
+                func=ACT.Exp,
+                scale=neg_tau[:, t : t + 1],
+            )
+
+        w2_q = quantize(weave_weight(w2_raw, "w2"), "w2")
+        square(0)
         for t in range(PACK):
-            sq = keep.tile([P, S], F32, name="sq%d" % t, tag="sq%d" % t)
-            nc.scalar.activation(out=sq[:], in_=low_banks[t][:], func=ACT.Square)
-            nc.scalar.copy(y[t][:], low_banks[t][:])
-            for h in range(2):
-                nc.scalar.activation(
-                    out=ea[t][:, halves[h]],
-                    in_=sq[:].indirect(n1_t[:, list_halves[h]]),
-                    func=ACT.Exp,
-                    scale=neg_tau[:, t : t + 1],
-                )
-            if t % 2 == 0:
-                weight_woven.append(weave_weight(weight_raw[t // 2], "w%d" % (2 + t // 2)))
+            if t < 2:
+                nc.scalar.copy(y[t], low_banks[t][:])
             else:
-                weight_q.append(quantize(weight_woven[t // 2], "w%d" % (2 + t // 2)))
-            for h in range(2):
-                nc.vector.scalar_tensor_tensor(
-                    u[t][:, halves[h]], low_banks[t][:, halves[h]], 2.0, ea[t][:, halves[h]], ALU.mult, ALU.mult
-                )
-            for h in range(2):
-                nc.vector.tensor_tensor(
-                    d[:, t, halves[h]], y[t][:].indirect(n2_t[:, list_halves[h]]), u[t][:, halves[h]], ALU.subtract
-                )
-        w2_q, w3_q = weight_q
+                nc.vector.tensor_copy(y[t], low_banks[t][:])
+            decay(t, 0)
+            if t + 1 < PACK:
+                square(t + 1)
+            decay(t, 1)
+            for cols, entries in pieces(t):
+                nc.vector.scalar_tensor_tensor(u[t][:, cols], low_banks[t][:, cols], 2.0, ea[t][:, cols], ALU.mult, ALU.mult)
+            for cols, entries in pieces(t):
+                nc.vector.tensor_tensor(d[:, t, cols], y_ea[t][:].indirect(n2_t[:, entries]), u[t][:, cols], ALU.subtract)
 
         gain_runs = neg_half_gn[:].unsqueeze(1).unsqueeze(3).to_broadcast([P, HALF // RUN, PACK, RUN])
-        z_woven = [keep.tile([P, PACK * HALF], BF16, name="z_woven%d" % h, align_bytes=64) for h in range(2)]
+        z_woven = [
+            keep.tile([P, PACK * HALF], BF16, name="z_woven%d" % h, tag="z_woven%d" % h, align_bytes=64) for h in range(2)
+        ]
         for h in range(2):
             nc.vector.tensor_tensor(woven_runs(z_woven[h]), by_runs(d, h), gain_runs, ALU.mult)
         high_banks = [psum.tile([P, S], F32, name="a_bank%d" % t, tag="high%d" % t) for t in range(PACK)]
@@ -186,29 +202,31 @@ def tile_picked_forkcxbegaebl_none_p_kernel(
                 product(high_banks[t], w2_q, t, h, z_q[h][0][:], z_q[h][1][:])
 
         sg = keep.tile([P, PACK, S], F32, name="sg", tag="sq%d" % (PACK - 1))
-        r = planes4("r")
+        r = keep.tile([P, PACK, S], F32, name="r", tag="z_woven1", align_bytes=64)
         v = keep.tile([P, PACK, S], F32, name="v")
         q = keep.tile([P, PACK, S], F32, name="q")
         for t in range(PACK):
-            for h in range(2):
-                gated(sg[:, t, halves[h]], y[t], n4_t, 0, t, h)
-            nc.scalar.activation(
-                out=r[t][:], in_=sg[:, t, :], func=ACT.Identity, scale=neg_gm[:, t : t + 1], bias=gm_t[:, t : t + 1]
-            )
+            gated(sg[:, t, :], y_ea[t], n4_t[:], 0, t)
             nc.vector.scalar_tensor_tensor(
                 v[:, t, :], low_banks[t][:], gm_t[:, t : t + 1], sg[:, t, :], ALU.mult, ALU.mult
             )
-            for h in range(2):
-                nc.vector.tensor_tensor(
-                    q[:, t, halves[h]], y[t][:].indirect(n3_t[:, list_halves[h]]), r[t][:, halves[h]], ALU.mult
-                )
-
-        a = planes4("a")
-        sg2 = planes4("sg2")
+            nc.gpsimd.tensor_scalar(
+                r[:, t, :], sg[:, t, :], neg_gm[:, t : t + 1], gm_t[:, t : t + 1], ALU.mult, ALU.add
+            )
+        w3_woven = keep.tile([P, PACK * S], BF16, name="w3_bf16", align_bytes=64)
+        nc.scalar.copy(
+            w3_woven[:].rearrange("p (t m j) -> p m j t", t=PACK, j=PACK),
+            w3_raw[:].rearrange("p j (m t) -> p m j t", t=PACK),
+        )
         for t in range(PACK):
-            nc.scalar.copy(a[t][:], high_banks[t][:])
-            for h in range(2):
-                gated(sg2[t][:, halves[h]], a[t], n5_t, 1, t, h)
+            for cols, entries in pieces(t):
+                nc.vector.tensor_tensor(q[:, t, cols], y_ea[t][:].indirect(n3_t[:, entries]), r[:, t, cols], ALU.mult)
+            if t == PACK - 2:
+                w3_q = quantize(w3_woven, "w3")
+
+        for t in range(PACK):
+            nc.scalar.copy(a[t], high_banks[t][:])
+            gated(sg2[t], a_u[t], n5_t[:], 1, t)
 
         z2_woven = [keep.tile([P, PACK * HALF], BF16, name="z2_woven%d" % h, align_bytes=64) for h in range(2)]
         for h in range(2):
@@ -219,22 +237,22 @@ def tile_picked_forkcxbegaebl_none_p_kernel(
             for h in range(2):
                 product(b_banks[t], w3_q, t, h, z2_q[h][0][:], z2_q[h][1][:])
 
-        b = planes4("b")
         sg3 = planes4("sg3")
         left = planes4("left")
         right = planes4("right")
         res = planes4("res")
         out_rows = out.rearrange("(p t) n -> p t n", t=PACK)
-        nc.scalar.copy(b[0][:], b_banks[0][:])
-        for t in (1, 0, 2, 3):
-            nc.vector.tensor_tensor(left[t][:], b_banks[t][:], sg2[t][:], ALU.mult)
+        nc.scalar.copy(b[0], b_banks[0][:])
+        for t in range(1, PACK):
+            nc.vector.tensor_copy(b[t], b_banks[t][:])
+        for t in range(2):
+            nc.gpsimd.tensor_tensor(left[t][:], b[t], sg2[t], ALU.mult)
         for t in range(PACK):
-            if t + 1 < PACK:
-                nc.scalar.copy(b[t + 1][:], b_banks[t + 1][:])
-            for h in range(2):
-                gated(sg3[t][:, halves[h]], b[t], n6_t, 2, t, h)
-            pieces = halves if t == PACK - 1 else [slice(0, S)]
-            for cols in pieces:
+            if t < 2:
+                nc.vector.tensor_tensor(left[t + 2][:], b_banks[t + 2][:], sg2[t + 2], ALU.mult)
+            for cols, entries in pieces(t):
+                gated(sg3[t][:, cols], b_sg2[t], n6_t[:, entries], 2, t)
                 nc.vector.tensor_tensor(right[t][:, cols], high_banks[t][:, cols], sg3[t][:, cols], ALU.mult)
-                nc.vector.tensor_tensor(res[t][:, cols], left[t][:, cols], right[t][:, cols], ALU.add)
+                adder = nc.gpsimd if t < 2 else nc.vector
+                adder.tensor_tensor(res[t][:, cols], left[t][:, cols], right[t][:, cols], ALU.add)
                 nc.sync.dma_start(out_rows[:, t, cols], res[t][:, cols])

@@ -40,20 +40,12 @@ def tile_picked_forkcxbegaebl_none_p_kernel(
             return tile
 
         def load_weight(dram, name):
-            raw = keep.tile([P, PACK, S], F32, name=name + "_raw")
+            raw = keep.tile([P, PACK, S], F32, name=name + "_raw", tag=name + "_raw")
             nc.sync.dma_start(raw[:], dram.rearrange("(p j) c -> p j c", j=PACK))
             return raw
 
         def load_rows(engine, dst, dram):
             engine.dma_start(dst, dram.rearrange("(p t) one -> p (t one)", t=PACK))
-
-        def weave_weight(raw, name):
-            woven = keep.tile([P, PACK * S], BF16, name=name + "_bf16", align_bytes=64)
-            nc.vector.tensor_copy(
-                out=woven[:].rearrange("p (t m j) -> p m j t", t=PACK, j=PACK),
-                in_=raw[:].rearrange("p j (m t) -> p m j t", t=PACK),
-            )
-            return woven
 
         def quantize(woven, name):
             width = woven.shape[1] // PACK
@@ -94,41 +86,38 @@ def tile_picked_forkcxbegaebl_none_p_kernel(
         xs = keep.tile([P, T], U8, name="xs")
         nc.gpsimd.memset(xs[:].bitcast(I32), 0)
         offs_t = load_list(offs, "offs_t")
+        n1_t = load_list(n1, "n1_t")
+        tau_t = keep.tile([P, PACK], F32, name="tau_t")
+        load_rows(nc.sync, tau_t[:], tau)
+        w1_raw = load_weight(w1, "w1")
         for q in range(4):
             nc.sync.dma_start(xs[32 * q : 32 * q + 4, :].bitcast(I32), x_scales[0, 4 * q : 4 * q + 4, :].bitcast(I32))
-        w1_raw = load_weight(w1, "w1")
         xw = keep.tile([P, T], U32, name="xw")
         nc.sync.dma_start(xw[:].bitcast(I32), x_words[0].rearrange("p c r -> p (c r)").bitcast(I32))
-        tau_t = keep.tile([P, PACK], F32, name="tau_t")
-        load_rows(nc.scalar, tau_t[:], tau)
-        n1_t = load_list(n1, "n1_t")
         w2_raw = load_weight(w2, "w2")
         n2_t = load_list(n2, "n2_t")
-        w3_raw = load_weight(w3, "w3")
         n4_t = load_list(n4, "n4_t")
-        n3_t = load_list(n3, "n3_t")
-        gn_t = keep.tile([P, PACK], F32, name="gn_t")
-        gm_t = keep.tile([P, PACK], F32, name="gm_t")
-        load_rows(nc.sync, gn_t[:], gn)
-        load_rows(nc.sync, gm_t[:], gm)
         slopes = keep.tile([P, 3, 8], F32, name="slopes")
         thresholds = keep.tile([P, 3, 8], F32, name="thresholds")
-        for g, (slope, threshold) in enumerate(((sl, th), (sl2, th2), (sl3, th3))):
-            load_rows(nc.sync, slopes[:, g, 0:PACK], slope)
-            load_rows(nc.sync, thresholds[:, g, 0:PACK], threshold)
+        gn_t = keep.tile([P, PACK], F32, name="gn_t")
+        gm_t = keep.tile([P, PACK], F32, name="gm_t")
+        for dst, dram in ((slopes[:, 0, 0:PACK], sl), (thresholds[:, 0, 0:PACK], th), (gn_t[:], gn), (gm_t[:], gm)):
+            load_rows(nc.sync, dst, dram)
+        with nc.allow_non_contiguous_dma(reason="one value a row of a or b, row 128 t + p to partition p"):
+            for g, (slope, threshold) in enumerate(((sl2, th2), (sl3, th3))):
+                nc.sync.dma_start(slopes[:, g + 1, 0:PACK], slope.rearrange("(t p) one -> p (t one)", p=P))
+                nc.sync.dma_start(thresholds[:, g + 1, 0:PACK], threshold.rearrange("(t p) one -> p (t one)", p=P))
+        w3_raw = load_weight(w3, "w3")
+        n3_t = load_list(n3, "n3_t")
         n5_t = load_list(n5, "n5_t")
         n6_t = load_list(n6, "n6_t")
 
-        neg_tau = keep.tile([P, PACK], F32, name="neg_tau")
-        nc.scalar.activation(out=neg_tau[:], in_=tau_t[:], func=ACT.Copy, scale=-1.0)
-        neg_half_gn = keep.tile([P, PACK], F32, name="neg_half_gn")
-        nc.gpsimd.tensor_scalar(neg_half_gn[:], gn_t[:], -0.5, 0.0, ALU.mult, ALU.add)
-        neg_gm = keep.tile([P, PACK], F32, name="neg_gm")
-        nc.gpsimd.tensor_scalar(neg_gm[:], gm_t[:], -1.0, 0.0, ALU.mult, ALU.add)
         neg_th = keep.tile([P, 3, PACK], F32, name="neg_th")
         nc.gpsimd.tensor_scalar(neg_th[:], thresholds[:, :, 0:PACK], -1.0, 0.0, ALU.mult, ALU.add)
         biases = keep.tile([P, 3, PACK], F32, name="biases")
         nc.gpsimd.tensor_tensor(biases[:], neg_th[:], slopes[:, :, 0:PACK], ALU.mult)
+        neg_half_gn = keep.tile([P, PACK], F32, name="neg_half_gn")
+        nc.gpsimd.tensor_scalar(neg_half_gn[:], gn_t[:], -0.5, 0.0, ALU.mult, ALU.add)
 
         def gated(dst, window, offsets, g, t):
             nc.scalar.activation(
@@ -139,19 +128,31 @@ def tile_picked_forkcxbegaebl_none_p_kernel(
                 bias=biases[:, g, t : t + 1],
             )
 
+        w1_woven = [keep.tile([P, 2 * S], BF16, name="w1_bf16_%d" % g, align_bytes=64) for g in range(2)]
+        w1_src = w1_raw[:].rearrange("p j (m t) -> p m j t", t=PACK)
+        nc.vector.tensor_copy(w1_woven[0][:].rearrange("p (t m j) -> p m j t", t=2, j=PACK), w1_src[:, :, :, 0:2])
+        nc.scalar.copy(w1_woven[1][:].rearrange("p (t m j) -> p m j t", t=2, j=PACK), w1_src[:, :, :, 2:4])
+        neg_tau = keep.tile([P, PACK], F32, name="neg_tau")
+        nc.scalar.activation(out=neg_tau[:], in_=tau_t[:], func=ACT.Copy, scale=-1.0)
         xs_g = keep.tile([P, S], U8, name="xs_g", align_bytes=64)
         nc.vector.tensor_copy(xs_g[:], xs[:].indirect(offs_t[:]))
-        w1_q = quantize(weave_weight(w1_raw, "w1"), "w1")
+        w1_q = [quantize(w1_woven[g], "w1_%d" % g) for g in range(2)]
         xw_g = keep.tile([P, S], U32, name="xw_g", align_bytes=64)
         low_banks = [psum.tile([P, S], F32, name="y_bank%d" % t, tag="low%d" % t) for t in range(PACK)]
         for h in range(2):
             nc.vector.tensor_copy(xw_g[:, halves[h]], xw[:].indirect(offs_t[:, list_halves[h]]))
         for t in range(PACK):
             for h in range(2):
-                product(low_banks[t], w1_q, t, h, xw_g[:, halves[h]], xs_g[:, halves[h]])
+                product(low_banks[t], w1_q[t // 2], t % 2, h, xw_g[:, halves[h]], xs_g[:, halves[h]])
 
+        w2_woven = keep.tile([P, PACK * S], BF16, name="w2_bf16", align_bytes=64)
+        nc.vector.tensor_copy(
+            w2_woven[:].rearrange("p (c i j) -> p c j i", i=RUN, j=PACK),
+            w2_raw[:].rearrange("p j (c i) -> p c j i", i=RUN),
+        )
         y_ea = pairs4("y_ea")
-        a_u = pairs4("a_u")
+        a_u = [keep.tile([P, 2 * S], F32, name="a_u0", tag="w2_raw")]
+        a_u = a_u + [keep.tile([P, 2 * S], F32, name="a_u%d" % t) for t in range(1, PACK)]
         b_sg2 = pairs4("b_sg2")
         y = [pair[:, 0:S] for pair in y_ea]
         ea = [pair[:, S : 2 * S] for pair in y_ea]
@@ -159,8 +160,8 @@ def tile_picked_forkcxbegaebl_none_p_kernel(
         u = [pair[:, S : 2 * S] for pair in a_u]
         b = [pair[:, 0:S] for pair in b_sg2]
         sg2 = [pair[:, S : 2 * S] for pair in b_sg2]
-        d = keep.tile([P, PACK, S], F32, name="d")
-        sq = [keep.tile([P, S], F32, name="sq%d" % t, tag="sq%d" % t) for t in range(PACK)]
+        d = keep.tile([P, PACK, S], F32, name="d", tag="d")
+        sq = [keep.tile([P, S], F32, name="sq%d" % t, tag="sq%d" % (t % 2)) for t in range(PACK)]
 
         def square(t):
             nc.scalar.activation(out=sq[t][:], in_=low_banks[t][:], func=ACT.Square)
@@ -173,21 +174,22 @@ def tile_picked_forkcxbegaebl_none_p_kernel(
                 scale=neg_tau[:, t : t + 1],
             )
 
-        w2_q = quantize(weave_weight(w2_raw, "w2"), "w2")
         square(0)
+        for t in (1, 0):
+            nc.vector.tensor_copy(y[t], low_banks[t][:])
         for t in range(PACK):
-            if t < 2:
+            if t >= 2:
                 nc.scalar.copy(y[t], low_banks[t][:])
-            else:
-                nc.vector.tensor_copy(y[t], low_banks[t][:])
-            decay(t, 0)
+            for h in range(2):
+                decay(t, h)
             if t + 1 < PACK:
                 square(t + 1)
-            decay(t, 1)
             for cols, entries in pieces(t):
                 nc.vector.scalar_tensor_tensor(u[t][:, cols], low_banks[t][:, cols], 2.0, ea[t][:, cols], ALU.mult, ALU.mult)
             for cols, entries in pieces(t):
                 nc.vector.tensor_tensor(d[:, t, cols], y_ea[t][:].indirect(n2_t[:, entries]), u[t][:, cols], ALU.subtract)
+            if t == 0:
+                w2_q = quantize(w2_woven, "w2")
 
         gain_runs = neg_half_gn[:].unsqueeze(1).unsqueeze(3).to_broadcast([P, HALF // RUN, PACK, RUN])
         z_woven = [
@@ -201,9 +203,9 @@ def tile_picked_forkcxbegaebl_none_p_kernel(
             for h in range(2):
                 product(high_banks[t], w2_q, t, h, z_q[h][0][:], z_q[h][1][:])
 
-        sg = keep.tile([P, PACK, S], F32, name="sg", tag="sq%d" % (PACK - 1))
+        sg = keep.tile([P, PACK, S], F32, name="sg", tag="sq1")
         r = keep.tile([P, PACK, S], F32, name="r", tag="z_woven1", align_bytes=64)
-        v = keep.tile([P, PACK, S], F32, name="v")
+        v = keep.tile([P, PACK, S], F32, name="v", tag="d")
         q = keep.tile([P, PACK, S], F32, name="q")
         for t in range(PACK):
             gated(sg[:, t, :], y_ea[t], n4_t[:], 0, t)
@@ -211,12 +213,12 @@ def tile_picked_forkcxbegaebl_none_p_kernel(
                 v[:, t, :], low_banks[t][:], gm_t[:, t : t + 1], sg[:, t, :], ALU.mult, ALU.mult
             )
             nc.gpsimd.tensor_scalar(
-                r[:, t, :], sg[:, t, :], neg_gm[:, t : t + 1], gm_t[:, t : t + 1], ALU.mult, ALU.add
+                r[:, t, :], sg[:, t, :], -1.0, gm_t[:, t : t + 1], ALU.add, ALU.mult
             )
         w3_woven = keep.tile([P, PACK * S], BF16, name="w3_bf16", align_bytes=64)
         nc.scalar.copy(
-            w3_woven[:].rearrange("p (t m j) -> p m j t", t=PACK, j=PACK),
-            w3_raw[:].rearrange("p j (m t) -> p m j t", t=PACK),
+            w3_woven[:].rearrange("p (c i j) -> p c j i", i=RUN, j=PACK),
+            w3_raw[:].rearrange("p j (c i) -> p c j i", i=RUN),
         )
         for t in range(PACK):
             for cols, entries in pieces(t):
@@ -230,7 +232,7 @@ def tile_picked_forkcxbegaebl_none_p_kernel(
 
         z2_woven = [keep.tile([P, PACK * HALF], BF16, name="z2_woven%d" % h, align_bytes=64) for h in range(2)]
         for h in range(2):
-            nc.vector.tensor_tensor(woven_runs(z2_woven[h]), by_runs(q, h), by_runs(v, h), ALU.add)
+            nc.vector.tensor_tensor(woven_runs(z2_woven[h]), by_runs(v, h), by_runs(q, h), ALU.subtract)
         b_banks = [psum.tile([P, S], F32, name="b_bank%d" % t, tag="low%d" % t) for t in range(PACK)]
         z2_q = [quantize(z2_woven[h], "z2_%d" % h) for h in range(2)]
         for t in range(PACK):
@@ -241,7 +243,7 @@ def tile_picked_forkcxbegaebl_none_p_kernel(
         left = planes4("left")
         right = planes4("right")
         res = planes4("res")
-        out_rows = out.rearrange("(p t) n -> p t n", t=PACK)
+        out_rows = out.rearrange("(t p) n -> p t n", p=P)
         nc.scalar.copy(b[0], b_banks[0][:])
         for t in range(1, PACK):
             nc.vector.tensor_copy(b[t], b_banks[t][:])

@@ -86,12 +86,12 @@ def tile_picked_forkcxbegaebl_none_p_kernel(
         xs = keep.tile([P, T], U8, name="xs")
         nc.gpsimd.memset(xs[:].bitcast(I32), 0)
         offs_t = load_list(offs, "offs_t")
+        for q in range(4):
+            nc.sync.dma_start(xs[32 * q : 32 * q + 4, :].bitcast(I32), x_scales[0, 4 * q : 4 * q + 4, :].bitcast(I32))
+        w1_raw = load_weight(w1, "w1")
         n1_t = load_list(n1, "n1_t")
         tau_t = keep.tile([P, PACK], F32, name="tau_t")
         load_rows(nc.sync, tau_t[:], tau)
-        w1_raw = load_weight(w1, "w1")
-        for q in range(4):
-            nc.sync.dma_start(xs[32 * q : 32 * q + 4, :].bitcast(I32), x_scales[0, 4 * q : 4 * q + 4, :].bitcast(I32))
         xw = keep.tile([P, T], U32, name="xw")
         nc.sync.dma_start(xw[:].bitcast(I32), x_words[0].rearrange("p c r -> p (c r)").bitcast(I32))
         w2_raw = load_weight(w2, "w2")
@@ -101,12 +101,11 @@ def tile_picked_forkcxbegaebl_none_p_kernel(
         thresholds = keep.tile([P, 3, 8], F32, name="thresholds")
         gn_t = keep.tile([P, PACK], F32, name="gn_t")
         gm_t = keep.tile([P, PACK], F32, name="gm_t")
-        for dst, dram in ((slopes[:, 0, 0:PACK], sl), (thresholds[:, 0, 0:PACK], th), (gn_t[:], gn), (gm_t[:], gm)):
-            load_rows(nc.sync, dst, dram)
-        with nc.allow_non_contiguous_dma(reason="one value a row of a or b, row 128 t + p to partition p"):
-            for g, (slope, threshold) in enumerate(((sl2, th2), (sl3, th3))):
-                nc.sync.dma_start(slopes[:, g + 1, 0:PACK], slope.rearrange("(t p) one -> p (t one)", p=P))
-                nc.sync.dma_start(thresholds[:, g + 1, 0:PACK], threshold.rearrange("(t p) one -> p (t one)", p=P))
+        load_rows(nc.sync, gn_t[:], gn)
+        load_rows(nc.sync, gm_t[:], gm)
+        for g, (slope, threshold) in enumerate(((sl, th), (sl2, th2), (sl3, th3))):
+            load_rows(nc.sync, slopes[:, g, 0:PACK], slope)
+            load_rows(nc.sync, thresholds[:, g, 0:PACK], threshold)
         w3_raw = load_weight(w3, "w3")
         n3_t = load_list(n3, "n3_t")
         n5_t = load_list(n5, "n5_t")
@@ -147,8 +146,8 @@ def tile_picked_forkcxbegaebl_none_p_kernel(
 
         w2_woven = keep.tile([P, PACK * S], BF16, name="w2_bf16", align_bytes=64)
         nc.vector.tensor_copy(
-            w2_woven[:].rearrange("p (c i j) -> p c j i", i=RUN, j=PACK),
-            w2_raw[:].rearrange("p j (c i) -> p c j i", i=RUN),
+            w2_woven[:].rearrange("p (t m j) -> p m j t", t=PACK, j=PACK),
+            w2_raw[:].rearrange("p j (m t) -> p m j t", t=PACK),
         )
         y_ea = pairs4("y_ea")
         a_u = [keep.tile([P, 2 * S], F32, name="a_u0", tag="w2_raw")]
@@ -217,8 +216,8 @@ def tile_picked_forkcxbegaebl_none_p_kernel(
             )
         w3_woven = keep.tile([P, PACK * S], BF16, name="w3_bf16", align_bytes=64)
         nc.scalar.copy(
-            w3_woven[:].rearrange("p (c i j) -> p c j i", i=RUN, j=PACK),
-            w3_raw[:].rearrange("p j (c i) -> p c j i", i=RUN),
+            w3_woven[:].rearrange("p (t m j) -> p m j t", t=PACK, j=PACK),
+            w3_raw[:].rearrange("p j (m t) -> p m j t", t=PACK),
         )
         for t in range(PACK):
             for cols, entries in pieces(t):
@@ -243,7 +242,7 @@ def tile_picked_forkcxbegaebl_none_p_kernel(
         left = planes4("left")
         right = planes4("right")
         res = planes4("res")
-        out_rows = out.rearrange("(t p) n -> p t n", p=P)
+        out_rows = out.rearrange("(p t) n -> p t n", t=PACK)
         nc.scalar.copy(b[0], b_banks[0][:])
         for t in range(1, PACK):
             nc.vector.tensor_copy(b[t], b_banks[t][:])

from contextlib import ExitStack

import concourse.mybir as mybir

F32 = mybir.dt.float32
BF16 = mybir.dt.bfloat16
I32 = mybir.dt.int32
U32 = mybir.dt.uint32
U16 = mybir.dt.uint16
U8 = mybir.dt.uint8
FP8X4 = mybir.dt.float8_e4m3fn_x4
ALU = mybir.AluOpType
ACT = mybir.ActivationFunctionType

P = 128
PACK = 4
T = 2048
S = 512
HALF = S // 2
LIST_COLS = S // 16
RUN = 4
FLOPS = 3 * 2 * 512 * 512 * 512


def tile_picked_forkcxbegaebl_none_p_kernel(
    tc, x_words, x_scales, w1, tau, sl, th, gn, w2, gm, w3, sl2, th2, sl3, th3, offs, n1, n2, n3, n4, n5, n6, out
):
    nc = tc.nc
    halves = [slice(h * HALF, (h + 1) * HALF) for h in range(2)]
    list_halves = [slice(h * LIST_COLS // 2, (h + 1) * LIST_COLS // 2) for h in range(2)]

    with ExitStack() as ctx:
        lists = ctx.enter_context(tc.tile_pool(name="lists", bufs=1))
        keep = ctx.enter_context(tc.tile_pool(name="keep", bufs=1))
        psum = ctx.enter_context(tc.psum_pool(name="psum", bufs=1))

        def load_list(dram, name):
            tile = lists.tile([P, LIST_COLS], U16, name=name)
            nc.sync.dma_start(tile[:], dram)
            return tile

        def load_weight(dram, name):
            raw = keep.tile([P, PACK, S], F32, name=name + "_raw", tag=name + "_raw")
            nc.sync.dma_start(raw[:], dram.rearrange("(p j) c -> p j c", j=PACK))
            return raw

        def load_rows(engine, dst, dram):
            engine.dma_start(dst, dram.rearrange("(p t) one -> p (t one)", t=PACK))

        def quantize(woven, name):
            width = woven.shape[1] // PACK
            codes = keep.tile([P, width], U32, name=name + "_codes", align_bytes=64)
            scales = keep.tile([P, width], U8, name=name + "_scales", align_bytes=64)
            nc.vector.quantize_mx(out=codes[:].bitcast(FP8X4), scales=scales[:], in_=woven[:])
            return codes, scales

        def product(bank, weight, t, h, codes, scales):
            cols = slice(t * P, (t + 1) * P)
            nc.tensor.matmul_mx(
                out=bank[:, halves[h]],
                lhsT=weight[0][:, cols].bitcast(FP8X4),
                lhsT_scale=weight[1][:, cols],
                rhs=codes.bitcast(FP8X4),
                rhs_scale=scales,
                start=True,
                stop=True,
            )

        def by_runs(planes, h):
            return planes[:, :, halves[h]].rearrange("p t (c i) -> p c t i", i=RUN)

        def woven_runs(woven):
            return woven[:].rearrange("p (c i t) -> p c t i", i=RUN, t=PACK)

        def planes4(name):
            return [keep.tile([P, S], F32, name="%s%d" % (name, t)) for t in range(PACK)]

        def pairs4(name):
            return [keep.tile([P, 2 * S], F32, name="%s%d" % (name, t)) for t in range(PACK)]

        def pieces(t):
            if t == PACK - 1:
                return list(zip(halves, list_halves))
            return [(slice(0, S), slice(0, LIST_COLS))]

        xs = keep.tile([P, T], U8, name="xs")
        nc.gpsimd.memset(xs[:].bitcast(I32), 0)
        offs_t = load_list(offs, "offs_t")
        for q in range(4):
            nc.sync.dma_start(xs[32 * q : 32 * q + 4, :].bitcast(I32), x_scales[0, 4 * q : 4 * q + 4, :].bitcast(I32))
        w1_raw = load_weight(w1, "w1")
        n1_t = load_list(n1, "n1_t")
        tau_t = keep.tile([P, PACK], F32, name="tau_t")
        load_rows(nc.sync, tau_t[:], tau)
        xw = keep.tile([P, T], U32, name="xw")
        nc.sync.dma_start(xw[:].bitcast(I32), x_words[0].rearrange("p c r -> p (c r)").bitcast(I32))
        w2_raw = load_weight(w2, "w2")
        n2_t = load_list(n2, "n2_t")
        n4_t = load_list(n4, "n4_t")
        slopes = keep.tile([P, 3, 8], F32, name="slopes")
        thresholds = keep.tile([P, 3, 8], F32, name="thresholds")
        gn_t = keep.tile([P, PACK], F32, name="gn_t")
        gm_t = keep.tile([P, PACK], F32, name="gm_t")
        load_rows(nc.sync, gn_t[:], gn)
        load_rows(nc.sync, gm_t[:], gm)
        for g, (slope, threshold) in enumerate(((sl, th), (sl2, th2), (sl3, th3))):
            load_rows(nc.sync, slopes[:, g, 0:PACK], slope)
            load_rows(nc.sync, thresholds[:, g, 0:PACK], threshold)
        w3_raw = load_weight(w3, "w3")
        n3_t = load_list(n3, "n3_t")
        n5_t = load_list(n5, "n5_t")
        n6_t = load_list(n6, "n6_t")

        neg_th = keep.tile([P, 3, PACK], F32, name="neg_th")
        nc.gpsimd.tensor_scalar(neg_th[:], thresholds[:, :, 0:PACK], -1.0, 0.0, ALU.mult, ALU.add)
        biases = keep.tile([P, 3, PACK], F32, name="biases")
        nc.gpsimd.tensor_tensor(biases[:], neg_th[:], slopes[:, :, 0:PACK], ALU.mult)
        neg_half_gn = keep.tile([P, PACK], F32, name="neg_half_gn")
        nc.gpsimd.tensor_scalar(neg_half_gn[:], gn_t[:], -0.5, 0.0, ALU.mult, ALU.add)

        def gated(dst, window, offsets, g, t):
            nc.scalar.activation(
                out=dst,
                in_=window[:].indirect(offsets),
                func=ACT.Sigmoid,
                scale=slopes[:, g, t : t + 1],
                bias=biases[:, g, t : t + 1],
            )

        w1_woven = [keep.tile([P, 2 * S], BF16, name="w1_bf16_%d" % g, align_bytes=64) for g in range(2)]
        w1_src = w1_raw[:].rearrange("p j (m t) -> p m j t", t=PACK)
        nc.vector.tensor_copy(w1_woven[0][:].rearrange("p (t m j) -> p m j t", t=2, j=PACK), w1_src[:, :, :, 0:2])
        nc.scalar.copy(w1_woven[1][:].rearrange("p (t m j) -> p m j t", t=2, j=PACK), w1_src[:, :, :, 2:4])
        neg_tau = keep.tile([P, PACK], F32, name="neg_tau")
        nc.scalar.activation(out=neg_tau[:], in_=tau_t[:], func=ACT.Copy, scale=-1.0)
        xs_g = keep.tile([P, S], U8, name="xs_g", align_bytes=64)
        nc.vector.tensor_copy(xs_g[:], xs[:].indirect(offs_t[:]))
        w1_q = [quantize(w1_woven[g], "w1_%d" % g) for g in range(2)]
        xw_g = keep.tile([P, S], U32, name="xw_g", align_bytes=64)
        low_banks = [psum.tile([P, S], F32, name="y_bank%d" % t, tag="low%d" % t) for t in range(PACK)]
        for h in range(2):
            nc.vector.tensor_copy(xw_g[:, halves[h]], xw[:].indirect(offs_t[:, list_halves[h]]))
        for t in range(PACK):
            for h in range(2):
                product(low_banks[t], w1_q[t // 2], t % 2, h, xw_g[:, halves[h]], xs_g[:, halves[h]])

        w2_woven = keep.tile([P, PACK * S], BF16, name="w2_bf16", align_bytes=64)
        nc.vector.tensor_copy(
            w2_woven[:].rearrange("p (t m j) -> p m j t", t=PACK, j=PACK),
            w2_raw[:].rearrange("p j (m t) -> p m j t", t=PACK),
        )
        y_ea = pairs4("y_ea")
        a_u = [keep.tile([P, 2 * S], F32, name="a_u0", tag="w2_raw")]
        a_u = a_u + [keep.tile([P, 2 * S], F32, name="a_u%d" % t) for t in range(1, PACK)]
        b_sg2 = pairs4("b_sg2")
        y = [pair[:, 0:S] for pair in y_ea]
        ea = [pair[:, S : 2 * S] for pair in y_ea]
        a = [pair[:, 0:S] for pair in a_u]
        u = [pair[:, S : 2 * S] for pair in a_u]
        b = [pair[:, 0:S] for pair in b_sg2]
        sg2 = [pair[:, S : 2 * S] for pair in b_sg2]
        d = keep.tile([P, PACK, S], F32, name="d", tag="d")
        sq = [keep.tile([P, S], F32, name="sq%d" % t, tag="sq%d" % (t % 2)) for t in range(PACK)]

        def square(t):
            nc.scalar.activation(out=sq[t][:], in_=low_banks[t][:], func=ACT.Square)

        def decay(t, h):
            nc.scalar.activation(
                out=ea[t][:, halves[h]],
                in_=sq[t][:].indirect(n1_t[:, list_halves[h]]),
                func=ACT.Exp,
                scale=neg_tau[:, t : t + 1],
            )

        square(0)
        for t in (1, 0):
            nc.vector.tensor_copy(y[t], low_banks[t][:])
        for t in range(PACK):
            if t >= 2:
                nc.scalar.copy(y[t], low_banks[t][:])
            for h in range(2):
                decay(t, h)
            if t + 1 < PACK:
                square(t + 1)
            for cols, entries in pieces(t):
                nc.vector.scalar_tensor_tensor(u[t][:, cols], low_banks[t][:, cols], 2.0, ea[t][:, cols], ALU.mult, ALU.mult)
            for cols, entries in pieces(t):
                nc.vector.tensor_tensor(d[:, t, cols], y_ea[t][:].indirect(n2_t[:, entries]), u[t][:, cols], ALU.subtract)
            if t == 0:
                w2_q = quantize(w2_woven, "w2")

        gain_runs = neg_half_gn[:].unsqueeze(1).unsqueeze(3).to_broadcast([P, HALF // RUN, PACK, RUN])
        z_woven = [
            keep.tile([P, PACK * HALF], BF16, name="z_woven%d" % h, tag="z_woven%d" % h, align_bytes=64) for h in range(2)
        ]
        for h in range(2):
            nc.vector.tensor_tensor(woven_runs(z_woven[h]), by_runs(d, h), gain_runs, ALU.mult)
        high_banks = [psum.tile([P, S], F32, name="a_bank%d" % t, tag="high%d" % t) for t in range(PACK)]
        z_q = [quantize(z_woven[h], "z%d" % h) for h in range(2)]
        for t in range(PACK):
            for h in range(2):
                product(high_banks[t], w2_q, t, h, z_q[h][0][:], z_q[h][1][:])

        sg = keep.tile([P, PACK, S], F32, name="sg", tag="sq1")
        r = keep.tile([P, PACK, S], F32, name="r", tag="z_woven1", align_bytes=64)
        v = keep.tile([P, PACK, S], F32, name="v", tag="d")
        q = keep.tile([P, PACK, S], F32, name="q")
        for t in range(PACK):
            gated(sg[:, t, :], y_ea[t], n4_t[:], 0, t)
            nc.vector.scalar_tensor_tensor(
                v[:, t, :], low_banks[t][:], gm_t[:, t : t + 1], sg[:, t, :], ALU.mult, ALU.mult
            )
            nc.gpsimd.tensor_scalar(
                r[:, t, :], sg[:, t, :], -1.0, gm_t[:, t : t + 1], ALU.add, ALU.mult
            )
        w3_woven = keep.tile([P, PACK * S], BF16, name="w3_bf16", align_bytes=64)
        nc.scalar.copy(
            w3_woven[:].rearrange("p (t m j) -> p m j t", t=PACK, j=PACK),
            w3_raw[:].rearrange("p j (m t) -> p m j t", t=PACK),
        )
        for t in range(PACK):
            for cols, entries in pieces(t):
                nc.vector.tensor_tensor(q[:, t, cols], y_ea[t][:].indirect(n3_t[:, entries]), r[:, t, cols], ALU.mult)
            if t == PACK - 2:
                w3_q = quantize(w3_woven, "w3")

        for t in range(PACK):
            nc.scalar.copy(a[t], high_banks[t][:])
            gated(sg2[t], a_u[t], n5_t[:], 1, t)

        z2_woven = [keep.tile([P, PACK * HALF], BF16, name="z2_woven%d" % h, align_bytes=64) for h in range(2)]
        for h in range(2):
            nc.vector.tensor_tensor(woven_runs(z2_woven[h]), by_runs(v, h), by_runs(q, h), ALU.subtract)
        b_banks = [psum.tile([P, S], F32, name="b_bank%d" % t, tag="low%d" % t) for t in range(PACK)]
        z2_q = [quantize(z2_woven[h], "z2_%d" % h) for h in range(2)]
        for t in range(PACK):
            for h in range(2):
                product(b_banks[t], w3_q, t, h, z2_q[h][0][:], z2_q[h][1][:])

        sg3 = planes4("sg3")
        left = planes4("left")
        right = planes4("right")
        res = planes4("res")
        out_rows = out.rearrange("(p t) n -> p t n", t=PACK)
        nc.scalar.copy(b[0], b_banks[0][:])
        for t in range(1, PACK):
            nc.vector.tensor_copy(b[t], b_banks[t][:])
        for t in range(2):
            nc.gpsimd.tensor_tensor(left[t][:], b[t], sg2[t], ALU.mult)
        for t in range(PACK):
            if t < 2:
                nc.vector.tensor_tensor(left[t + 2][:], b_banks[t + 2][:], sg2[t + 2], ALU.mult)
            for cols, entries in pieces(t):
                gated(sg3[t][:, cols], b_sg2[t], n6_t[:, entries], 2, t)
                nc.vector.tensor_tensor(right[t][:, cols], high_banks[t][:, cols], sg3[t][:, cols], ALU.mult)
                adder = nc.gpsimd if t < 2 else nc.vector
                adder.tensor_tensor(res[t][:, cols], left[t][:, cols], right[t][:, cols], ALU.add)
                nc.sync.dma_start(out_rows[:, t, cols], res[t][:, cols])
